import numpy as np
import ml_dtypes

BF16 = ml_dtypes.bfloat16


def bf(x):
    return np.asarray(x, np.float32).astype(BF16)


def f32(x):
    return np.asarray(x, np.float32)


def f64(x):
    return np.asarray(x).astype(np.float64)


def striped(idx):
    return np.tile(idx.reshape(-1, 16).T, (8, 1))


S, K, M, N, B, Q = 512, 128, 128, 128, 2, 64


def gelu_tanh(v):
    return 0.5 * v * (1.0 + np.tanh(np.sqrt(2.0 / np.pi) * (v + 0.044715 * v**3)))


def setup_inputs():
    return {"base": bf(np.random.standard_normal((B, M, S))), "x": bf(np.random.standard_normal((K, N))), "w": bf(np.random.standard_normal((K, M)) / np.sqrt(K)), "b": f32(0.5 * np.random.standard_normal((M, 1))), "offs": striped(np.random.permutation(S)[:N])}


def reference(base, x, w, b, offs):
    idx = offs[:16].T.reshape(-1)
    z = f64(base).copy()
    for i in range(B):
        z[i][:, idx[i * Q : (i + 1) * Q]] = f64(w).T @ f64(x)[:, i * Q : (i + 1) * Q]
    return gelu_tanh(z + f64(b))

@@ -1,0 +1,58 @@
+import concourse.mybir as mybir
+from concourse.masks import make_identity
+
+BF16, F32, U16 = mybir.dt.bfloat16, mybir.dt.float32, mybir.dt.uint16
+GELU_TANH = mybir.ActivationFunctionType.Gelu_apprx_tanh
+
+SEQUENCES, FEATURES, TOKENS = 2, 128, 512
+K = 128
+PIECE = 64
+N = SEQUENCES * PIECE
+LIST_COLUMNS = PIECE // 16
+
+FLOPS = 2 * K * FEATURES * N
+
+
+def tile_scatter_matmul_kernel(tc, base, x, w, b, offs, out):
+    nc = tc.nc
+    with (
+        tc.tile_pool(name="held", bufs=1) as held,
+        tc.psum_pool(name="psum", bufs=1) as psum,
+    ):
+        base_tiles = []
+        for i in range(SEQUENCES):
+            base_tile = held.tile([FEATURES, TOKENS], BF16, name=f"base{i}")
+            nc.sync.dma_start(base_tile[:], base[i])
+            base_tiles.append(base_tile)
+        w_tile = held.tile([K, FEATURES], BF16, name="w_tile")
+        nc.sync.dma_start(w_tile[:], w)
+        x_tile = held.tile([K, N], BF16, name="x_tile")
+        nc.sync.dma_start(x_tile[:], x)
+        offsets = held.tile([128, N // 16], U16, name="offsets")
+        nc.sync.dma_start(offsets[:], offs)
+        bias = held.tile([FEATURES, 1], F32, name="bias")
+        nc.scalar.dma_start(bias[:], b)
+
+        identity = held.tile([128, 128], BF16, name="identity")
+        make_identity(nc, identity[:])
+
+        windows = []
+        for i in range(SEQUENCES):
+            window = psum.tile([FEATURES, TOKENS], F32, name=f"window{i}")
+            nc.tensor.matmul(window[:], identity[:], base_tiles[i][:], start=True, stop=True)
+            windows.append(window)
+
+        for i in range(SEQUENCES):
+            piece = offsets[:, i * LIST_COLUMNS : (i + 1) * LIST_COLUMNS]
+            nc.tensor.matmul(
+                windows[i][:].indirect(piece),
+                w_tile[:],
+                x_tile[:, i * PIECE : (i + 1) * PIECE],
+                start=True,
+                stop=True,
+            )
+
+        for i in range(SEQUENCES):
+            result = held.tile([FEATURES, TOKENS], F32, name=f"result{i}")
+            nc.scalar.activation(result[:], windows[i][:], GELU_TANH, bias=bias[:])
+            nc.sync.dma_start(out[i], result[:])

@@ -33,6 +33,11 @@ def tile_scatter_matmul_kernel(tc, base, x, w, b, offs, out):
         bias = held.tile([FEATURES, 1], F32, name="bias")
         nc.scalar.dma_start(bias[:], b)
 
+        zero = held.tile([128, 1], F32, name="zero")
+        nc.vector.memset(zero[:], 0.0)
+        table_call = held.tile([128, 1], F32, name="table_call")
+        nc.scalar.activation(table_call[:], zero[:], GELU_TANH, bias=zero[:])
+
         identity = held.tile([128, 128], BF16, name="identity")
         make_identity(nc, identity[:])
 

@@ -8,6 +8,7 @@ SEQUENCES, FEATURES, TOKENS = 2, 128, 512
 K = 128
 PIECE = 64
 N = SEQUENCES * PIECE
+WARM_UPS = 3
 LIST_COLUMNS = PIECE // 16
 
 FLOPS = 2 * K * FEATURES * N
@@ -40,6 +41,12 @@ def tile_scatter_matmul_kernel(tc, base, x, w, b, offs, out):
 
         identity = held.tile([128, 128], BF16, name="identity")
         make_identity(nc, identity[:])
+
+        zeros = held.tile([128, TOKENS], BF16, name="zeros")
+        nc.vector.memset(zeros[:], 0.0)
+        warm_bank = psum.tile([128, TOKENS], F32, name="warm_bank")
+        for repeat in range(WARM_UPS):
+            nc.tensor.matmul(warm_bank[:], zeros[:, :128], zeros[:], start=True, stop=True)
 
         windows = []
         for i in range(SEQUENCES):

@@ -32,7 +32,7 @@ def tile_scatter_matmul_kernel(tc, base, x, w, b, offs, out):
         offsets = held.tile([128, N // 16], U16, name="offsets")
         nc.sync.dma_start(offsets[:], offs)
         bias = held.tile([FEATURES, 1], F32, name="bias")
-        nc.scalar.dma_start(bias[:], b)
+        nc.sync.dma_start(bias[:], b)
 
         zero = held.tile([128, 1], F32, name="zero")
         nc.vector.memset(zero[:], 0.0)

@@ -8,7 +8,8 @@ SEQUENCES, FEATURES, TOKENS = 2, 128, 512
 K = 128
 PIECE = 64
 N = SEQUENCES * PIECE
-WARM_UPS = 3
+WARM_COLUMNS = 128
+WARM_UPS = 14
 LIST_COLUMNS = PIECE // 16
 
 FLOPS = 2 * K * FEATURES * N
@@ -39,14 +40,14 @@ def tile_scatter_matmul_kernel(tc, base, x, w, b, offs, out):
         table_call = held.tile([128, 1], F32, name="table_call")
         nc.scalar.activation(table_call[:], zero[:], GELU_TANH, bias=zero[:])
 
+        zeros = held.tile([128, WARM_COLUMNS], BF16, name="zeros")
+        nc.gpsimd.memset(zeros[:], 0.0)
         identity = held.tile([128, 128], BF16, name="identity")
         make_identity(nc, identity[:])
 
-        zeros = held.tile([128, TOKENS], BF16, name="zeros")
-        nc.vector.memset(zeros[:], 0.0)
-        warm_bank = psum.tile([128, TOKENS], F32, name="warm_bank")
+        warm_bank = psum.tile([128, WARM_COLUMNS], F32, name="warm_bank")
         for repeat in range(WARM_UPS):
-            nc.tensor.matmul(warm_bank[:], zeros[:, :128], zeros[:], start=True, stop=True)
+            nc.tensor.matmul(warm_bank[:], zeros[:], zeros[:], start=True, stop=True)
 
         windows = []
         for i in range(SEQUENCES):

import concourse.mybir as mybir
from concourse.masks import make_identity

BF16, F32, U16 = mybir.dt.bfloat16, mybir.dt.float32, mybir.dt.uint16
GELU_TANH = mybir.ActivationFunctionType.Gelu_apprx_tanh

SEQUENCES, FEATURES, TOKENS = 2, 128, 512
K = 128
PIECE = 64
N = SEQUENCES * PIECE
WARM_COLUMNS = 128
WARM_UPS = 14
LIST_COLUMNS = PIECE // 16

FLOPS = 2 * K * FEATURES * N


def tile_scatter_matmul_kernel(tc, base, x, w, b, offs, out):
    nc = tc.nc
    with (
        tc.tile_pool(name="held", bufs=1) as held,
        tc.psum_pool(name="psum", bufs=1) as psum,
    ):
        base_tiles = []
        for i in range(SEQUENCES):
            base_tile = held.tile([FEATURES, TOKENS], BF16, name=f"base{i}")
            nc.sync.dma_start(base_tile[:], base[i])
            base_tiles.append(base_tile)
        w_tile = held.tile([K, FEATURES], BF16, name="w_tile")
        nc.sync.dma_start(w_tile[:], w)
        x_tile = held.tile([K, N], BF16, name="x_tile")
        nc.sync.dma_start(x_tile[:], x)
        offsets = held.tile([128, N // 16], U16, name="offsets")
        nc.sync.dma_start(offsets[:], offs)
        bias = held.tile([FEATURES, 1], F32, name="bias")
        nc.sync.dma_start(bias[:], b)

        zero = held.tile([128, 1], F32, name="zero")
        nc.vector.memset(zero[:], 0.0)
        table_call = held.tile([128, 1], F32, name="table_call")
        nc.scalar.activation(table_call[:], zero[:], GELU_TANH, bias=zero[:])

        zeros = held.tile([128, WARM_COLUMNS], BF16, name="zeros")
        nc.gpsimd.memset(zeros[:], 0.0)
        identity = held.tile([128, 128], BF16, name="identity")
        make_identity(nc, identity[:])

        warm_bank = psum.tile([128, WARM_COLUMNS], F32, name="warm_bank")
        for repeat in range(WARM_UPS):
            nc.tensor.matmul(warm_bank[:], zeros[:], zeros[:], start=True, stop=True)

        windows = []
        for i in range(SEQUENCES):
            window = psum.tile([FEATURES, TOKENS], F32, name=f"window{i}")
            nc.tensor.matmul(window[:], identity[:], base_tiles[i][:], start=True, stop=True)
            windows.append(window)

        for i in range(SEQUENCES):
            piece = offsets[:, i * LIST_COLUMNS : (i + 1) * LIST_COLUMNS]
            nc.tensor.matmul(
                windows[i][:].indirect(piece),
                w_tile[:],
                x_tile[:, i * PIECE : (i + 1) * PIECE],
                start=True,
                stop=True,
            )

        for i in range(SEQUENCES):
            result = held.tile([FEATURES, TOKENS], F32, name=f"result{i}")
            nc.scalar.activation(result[:], windows[i][:], GELU_TANH, bias=bias[:])
            nc.sync.dma_start(out[i], result[:])
